import numpy as np
import ml_dtypes


def mxq(x, axis, fmt="e4m3"):
    dtype, down = {"e4m3": (ml_dtypes.float8_e4m3fn, 7), "e5m2": (ml_dtypes.float8_e5m2, 14)}[fmt]
    v = np.moveaxis(np.asarray(x, np.float32).astype(ml_dtypes.bfloat16).astype(np.float64), axis, -1)
    blocks = v.reshape(v.shape[:-1] + (-1, 32))
    amax = np.abs(blocks).max(-1, keepdims=True)
    byte = np.maximum(np.where(amax > 0, np.frexp(amax)[1] - 1 + 127, 0) - down, 1)
    scale = np.exp2(byte - 127.0)
    codes = (blocks / scale).astype(np.float32).astype(dtype).astype(np.float64)
    return np.moveaxis((codes * scale).reshape(v.shape), -1, axis)


WIDE = False


def mx_kscale(k):
    if not WIDE:
        return np.ones(k)
    levels = np.array([30, -30])
    if k % 512:
        return np.exp2(np.random.permutation(np.resize(levels, k // 32))).repeat(32)
    a = np.empty((k // 512, 16))
    for p in range(k // 512):
        a[p, :8] = np.random.permutation(np.resize(levels, 8))
        for g in range(8):
            far = levels[np.abs(levels - a[p, g]) >= 10]
            a[p, g + 8] = far[np.random.randint(len(far))]
    return np.exp2(a.ravel()).repeat(32)


def f64(x):
    return np.asarray(x).astype(np.float64)


def striped(idx):
    return np.tile(np.asarray(idx).reshape(-1, 16).T, (8, 1)).astype(np.uint16)


def unstriped(offs):
    return offs[:16].T.reshape(-1).astype(np.int64)


E2M1 = np.array([0.0, 0.5, 1.0, 1.5, 2.0, 3.0, 4.0, 6.0, -0.0, -0.5, -1.0, -1.5, -2.0, -3.0, -4.0, -6.0])


def pack_weight(w, fmt):
    k, n = w.shape
    w = f64(np.asarray(w, np.float32).astype(ml_dtypes.bfloat16)).reshape(k // 32, 32, n)
    amax = np.abs(w).max(1)
    if fmt in ("e4m3", "e5m2"):
        byte = np.frexp(amax)[1] - 1 + 127 - (7 if fmt == "e4m3" else 14)
    else:
        mant, ex = np.frexp(amax / 6.0)
        byte = np.where(mant > 0.5, ex, ex - 1) + 127
    byte = np.clip(np.where(amax > 0, byte, 1), 1, 254)
    scaled = (w * np.exp2(127.0 - byte)[:, None, :]).reshape(k, n).astype(np.float32)
    by_word = np.ascontiguousarray(scaled.reshape(k // 512, 128, 4, n).transpose(0, 1, 3, 2))
    if fmt in ("e4m3", "e5m2"):
        words = by_word.astype(ml_dtypes.float8_e4m3fn if fmt == "e4m3" else ml_dtypes.float8_e5m2).view(np.uint8)
    else:
        c = by_word.astype(ml_dtypes.float4_e2m1fn).view(np.uint8) & 0xF
        words = (c[..., 0::2] | (c[..., 1::2] << 4)).reshape(k // 512, 128, 2 * n)
    return np.ascontiguousarray(words), np.ascontiguousarray(byte.astype(np.uint8).reshape(k // 512, 16, n))


def unpack_weight(words, scales, fmt):
    g, _, n = scales.shape
    words = np.ascontiguousarray(words).reshape(g, 128, n, -1)
    if fmt in ("e4m3", "e5m2"):
        vals = words.view(ml_dtypes.float8_e4m3fn if fmt == "e4m3" else ml_dtypes.float8_e5m2).astype(np.float64)
    else:
        nib = np.empty((g, 128, n, 4), np.uint8)
        nib[..., 0::2] = words & 0xF
        nib[..., 1::2] = words >> 4
        vals = E2M1[nib]
    vals = vals * np.repeat(np.exp2(scales.astype(np.float64) - 127.0), 8, axis=1)[..., None]
    return vals.transpose(0, 1, 3, 2).reshape(g * 512, n)


K, T, Z, J, R, C, N, L, E = 512, 1024, 1024, 256, 512, 512, 256, 512, 128


def setup_inputs():
    n = np.random.standard_normal
    idx = np.random.permutation(T)[:J]
    idx2 = np.random.permutation(Z)[:J]
    idx3 = np.random.permutation(C)[:J]
    idx4 = np.random.permutation(C)[:J]
    idx5 = np.random.permutation(J)[:E]
    idx6 = np.random.permutation(J)[:E]
    fk = mx_kscale(K)
    fr = mx_kscale(R)
    fl = mx_kscale(L)
    xtp = pack_weight(n((K, T)) / fk[:, None], "e4m3")
    xop = pack_weight(n((K, Z)) / fk[:, None], "e2m1")
    wp = pack_weight(n((K, R)) * 1 / np.sqrt(K) * fk[:, None] * fr, "e5m2")
    w2p = pack_weight(n((K, R)) * 1 / np.sqrt(K) * fk[:, None] * fr, "e5m2")
    wbp = pack_weight(n((R, N)) * 1 / np.sqrt(R) / fr[:, None], "e5m2")
    sxp = pack_weight(n((L, J)) / fl[:, None], "e2m1")
    wsp = pack_weight(n((L, N)) * 1 / np.sqrt(L) * fl[:, None], "e5m2")
    return {
        "xt_words": xtp[0],
        "xt_scales": xtp[1],
        "xo_words": xop[0],
        "xo_scales": xop[1],
        "w_words": wp[0],
        "w_scales": wp[1],
        "w2_words": w2p[0],
        "w2_scales": w2p[1],
        "wb_words": wbp[0],
        "wb_scales": wbp[1],
        "sx_words": sxp[0],
        "sx_scales": sxp[1],
        "ws_words": wsp[0],
        "ws_scales": wsp[1],
        "offs": striped(idx),
        "offs2": striped(idx2),
        "offs3": striped(idx3),
        "offs4": striped(idx4),
        "offs5": striped(idx5),
        "offs6": striped(idx6),
    }


def reference(xt_words, xt_scales, xo_words, xo_scales, w_words, w_scales, w2_words, w2_scales, wb_words, wb_scales, sx_words, sx_scales, ws_words, ws_scales, offs, offs2, offs3, offs4, offs5, offs6):
    idx = unstriped(offs)
    idx2 = unstriped(offs2)
    idx3 = unstriped(offs3)
    idx4 = unstriped(offs4)
    idx5 = unstriped(offs5)
    idx6 = unstriped(offs6)
    xtu = unpack_weight(xt_words, xt_scales, "e4m3")
    xou = unpack_weight(xo_words, xo_scales, "e2m1")
    wu = unpack_weight(w_words, w_scales, "e5m2")
    w2u = unpack_weight(w2_words, w2_scales, "e5m2")
    wbu = unpack_weight(wb_words, wb_scales, "e5m2")
    sxu = unpack_weight(sx_words, sx_scales, "e2m1")
    wsu = unpack_weight(ws_words, ws_scales, "e5m2")
    xtidxg = xtu[:, idx]
    xoidx2g = xou[:, idx2]
    a = wu.T @ xtidxg + w2u.T @ xoidx2g
    b = w2u.T @ xtidxg + wu.T @ xoidx2g
    pw = np.zeros((R, C))
    pw[:, idx3] = a
    hid = np.maximum(pw[:, idx4], b)
    hidq = mxq(hid, 0, "e4m3")
    p = wbu.T @ hidq + wsu.T @ sxu
    y = np.maximum(p[:, idx5], p[:, idx6])
    return y

@@ -1,0 +1,185 @@
+from contextlib import ExitStack
+
+import concourse.mybir as mybir
+
+K, T, Z, J, R, C, N, L, E = 512, 1024, 1024, 256, 512, 512, 256, 512, 128
+FLOPS = 2 * J * (4 * K * R + R * N + L * N)
+
+F32 = mybir.dt.float32
+BF16 = mybir.dt.bfloat16
+I32 = mybir.dt.int32
+U32 = mybir.dt.uint32
+U16 = mybir.dt.uint16
+U8 = mybir.dt.uint8
+E4M3 = mybir.dt.float8_e4m3fn_x4
+E5M2 = mybir.dt.float8_e5m2_x4
+E2M1 = mybir.dt.float4_e2m1fn_x4
+COPY = mybir.ActivationFunctionType.Copy
+MAX = mybir.AluOpType.max
+
+P = 128
+PACK = 4
+QUADS = 4
+
+
+def tile_list_crossed_board_skip_bestoftwo_kernel(
+    tc, xt_words, xt_scales, xo_words, xo_scales, w_words, w_scales, w2_words, w2_scales,
+    wb_words, wb_scales, sx_words, sx_scales, ws_words, ws_scales,
+    offs, offs2, offs3, offs4, offs5, offs6, out,
+):
+    nc = tc.nc
+    with ExitStack() as ctx:
+        sb = ctx.enter_context(tc.tile_pool(name="sb", bufs=1))
+        ps = ctx.enter_context(tc.psum_pool(name="ps", bufs=1))
+
+        def tile(name, shape, dtype):
+            return sb.tile(shape, dtype, name=name, align_bytes=64)
+
+        def load_list(name, src):
+            lst = sb.tile(list(src.shape), U16, name=name)
+            nc.sync.dma_start(lst[:], src)
+            return lst
+
+        def load_words(queue, dst, src):
+            rows = src[0]
+            if len(rows.shape) == 3:
+                rows = rows.rearrange("p n t -> p (n t)")
+            queue.dma_start(dst.bitcast(I32), rows.bitcast(I32))
+
+        def load_scales(dst, src):
+            rows = src[0].bitcast(I32)
+            for q in range(QUADS):
+                nc.sync.dma_start(dst[32 * q : 32 * q + 4, :].bitcast(I32), rows[4 * q : 4 * q + 4, :])
+
+        xt_w = tile("xt_w", [P, T], U32)
+        xt_s = tile("xt_s", [P, T], U8)
+        xo_w = tile("xo_w", [P, Z], U16)
+        xo_s = tile("xo_s", [P, Z], U8)
+        w_raw = tile("w_raw", [P, R], U32)
+        w2_raw = tile("w2_raw", [P, R], U32)
+        ws1_raw = tile("ws1_raw", [P, 2 * R], U8)
+        s2 = tile("s2", [P, 3 * N], U8)
+        boards = [tile("board%d" % t, [P, C], F32) for t in range(PACK)]
+
+        for plane in (xt_s, xo_s, ws1_raw, s2):
+            nc.vector.memset(plane[:].bitcast(I32), 0)
+        for board in boards:
+            nc.vector.memset(board[:], 0.0)
+
+        l1 = load_list("l1", offs)
+        l2 = load_list("l2", offs2)
+        load_words(nc.scalar, xt_w[:], xt_words)
+        load_words(nc.scalar, xo_w[:], xo_words)
+        load_words(nc.scalar, w_raw[:], w_words)
+        load_words(nc.scalar, w2_raw[:], w2_words)
+        load_scales(xt_s, xt_scales)
+        load_scales(xo_s, xo_scales)
+        load_scales(ws1_raw[:, 0:R], w_scales)
+        load_scales(ws1_raw[:, R : 2 * R], w2_scales)
+        l3 = load_list("l3", offs3)
+        l4 = load_list("l4", offs4)
+        wb_w = tile("wb_w", [P, N], U32)
+        ws_w = tile("ws_w", [P, N], U32)
+        sx_w = tile("sx_w", [P, J], U16)
+        wb_s, ws_s, sx_s = s2[:, 0:N], s2[:, N : 2 * N], s2[:, 2 * N : 3 * N]
+        load_words(nc.sync, sx_w[:], sx_words)
+        load_words(nc.sync, ws_w[:], ws_words)
+        load_scales(sx_s, sx_scales)
+        load_scales(ws_s, ws_scales)
+        load_words(nc.sync, wb_w[:], wb_words)
+        load_scales(wb_s, wb_scales)
+        l5 = load_list("l5", offs5)
+        l6 = load_list("l6", offs6)
+
+        xt_gs = tile("xt_gs", [P, J], U8)
+        xt_gw = tile("xt_gw", [P, J], U32)
+        xo_gs = tile("xo_gs", [P, J], U8)
+        xo_gw = tile("xo_gw", [P, J], U16)
+        w_w = tile("w_w", [P, R], U32)
+        w2_w = tile("w2_w", [P, R], U32)
+        w_s = tile("w_s", [P, R], U8)
+        w2_s = tile("w2_s", [P, R], U8)
+
+        def deal(copy, dst, src):
+            copy(dst.rearrange("p (t m) -> p t m", t=PACK), src.rearrange("p (m t) -> p t m", t=PACK))
+
+        nc.vector.tensor_copy(xt_gw[:], xt_w[:].indirect(l1[:]))
+        nc.vector.tensor_copy(xo_gw[:], xo_w[:].indirect(l2[:]))
+        nc.vector.tensor_copy(xt_gs[:], xt_s[:].indirect(l1[:]))
+        deal(nc.scalar.copy, w_w[:], w_raw[:])
+        deal(nc.vector.tensor_copy, w2_w[:], w2_raw[:])
+        nc.vector.tensor_copy(xo_gs[:], xo_s[:].indirect(l2[:]))
+        deal(nc.vector.tensor_copy, w_s[:], ws1_raw[:, 0:R])
+        deal(nc.vector.tensor_copy, w2_s[:], ws1_raw[:, R : 2 * R])
+
+        xt_op = (xt_gw[:].bitcast(E4M3), xt_gs[:])
+        xo_op = (xo_gw[:].bitcast(E2M1), xo_gs[:])
+
+        def mm(dst, words, scales, col0, moving, start, stop):
+            cols = slice(col0, col0 + P)
+            nc.tensor.matmul_mx(
+                out=dst, lhsT=words[:, cols].bitcast(E5M2), lhsT_scale=scales[:, cols],
+                rhs=moving[0], rhs_scale=moving[1], start=start, stop=stop,
+            )
+
+        order = (0, 2, 1, 3)
+        a_ps = [ps.tile([P, J], F32, name="a_ps%d" % t) for t in range(PACK)]
+        b_ps = [ps.tile([P, 2, J], F32, name="b_ps%d" % h) for h in range(2)]
+        p_ps = [ps.tile([P, J], F32, name="p_ps%d" % h) for h in range(2)]
+        for t in order:
+            mm(a_ps[t][:], w_w, w_s, t * P, xt_op, True, False)
+        for t in order:
+            mm(a_ps[t][:], w2_w, w2_s, t * P, xo_op, False, True)
+        for t in range(PACK):
+            mm(b_ps[t // 2][:, t % 2, :], w2_w, w2_s, t * P, xt_op, True, False)
+            mm(b_ps[t // 2][:, t % 2, :], w_w, w_s, t * P, xo_op, False, True)
+        sx_op = (sx_w[:].bitcast(E2M1), sx_s)
+        for h in range(2):
+            mm(p_ps[h][:], ws_w, ws_s, h * P, sx_op, True, False)
+
+        a_sb = [tile("a_sb%d" % t, [P, J], F32) for t in range(PACK)]
+        got = [tile("got%d" % h, [P, 2, J], F32) for h in range(2)]
+        hid = tile("hid", [P, J, PACK], BF16)
+
+        def larger(h):
+            nc.vector.tensor_tensor(
+                hid[:, :, 2 * h : 2 * h + 2],
+                got[h][:].rearrange("p t j -> p j t"),
+                b_ps[h][:].rearrange("p t j -> p j t"),
+                MAX,
+            )
+
+        for t in (0, 2, 1):
+            nc.scalar.activation(a_sb[t][:], a_ps[t][:], COPY)
+        nc.vector.tensor_copy(boards[0][:].indirect(l3[:]), a_sb[0][:])
+        nc.scalar.activation(boards[2][:].indirect(l3[:]), a_sb[2][:], COPY)
+        nc.vector.tensor_copy(boards[1][:].indirect(l3[:]), a_sb[1][:])
+        nc.scalar.activation(a_sb[3][:], a_ps[3][:], COPY)
+        nc.scalar.activation(boards[3][:].indirect(l3[:]), a_sb[3][:], COPY)
+        for t in (0, 1):
+            nc.vector.tensor_copy(got[0][:, t, :], boards[t][:].indirect(l4[:]))
+        for t in (2, 3):
+            nc.scalar.activation(got[1][:, t - 2, :], boards[t][:].indirect(l4[:]), COPY)
+        larger(0)
+        larger(1)
+
+        hid_w = tile("hid_w", [P, J], U32)
+        hid_s = tile("hid_s", [P, J], U8)
+        nc.vector.quantize_mx(out=hid_w[:].bitcast(E4M3), scales=hid_s[:], in_=hid[:].rearrange("p j t -> p (j t)"))
+        hid_op = (hid_w[:].bitcast(E4M3), hid_s[:])
+        for h in range(2):
+            mm(p_ps[h][:], wb_w, wb_s, h * P, hid_op, False, True)
+
+        p_sb = [tile("p_sb%d" % h, [P, J], F32) for h in range(2)]
+        first = [tile("first%d" % h, [P, E], F32) for h in range(2)]
+        second = [tile("second%d" % h, [P, E], F32) for h in range(2)]
+        best = [tile("best%d" % h, [P, E], F32) for h in range(2)]
+        nc.scalar.activation(p_sb[0][:], p_ps[0][:], COPY)
+        nc.vector.tensor_copy(p_sb[1][:], p_ps[1][:])
+        nc.scalar.activation(first[0][:], p_sb[0][:].indirect(l5[:]), COPY)
+        nc.scalar.activation(second[0][:], p_sb[0][:].indirect(l6[:]), COPY)
+        nc.vector.tensor_copy(first[1][:], p_sb[1][:].indirect(l5[:]))
+        nc.vector.tensor_copy(second[1][:], p_sb[1][:].indirect(l6[:]))
+        for h, queue in ((0, nc.scalar), (1, nc.sync)):
+            nc.vector.tensor_tensor(best[h][:], first[h][:], second[h][:], MAX)
+            queue.dma_start(out[h * P : (h + 1) * P, :], best[h][:])

@@ -32,8 +32,8 @@ def tile_list_crossed_board_skip_bestoftwo_kernel(
         sb = ctx.enter_context(tc.tile_pool(name="sb", bufs=1))
         ps = ctx.enter_context(tc.psum_pool(name="ps", bufs=1))
 
-        def tile(name, shape, dtype):
-            return sb.tile(shape, dtype, name=name, align_bytes=64)
+        def tile(name, shape, dtype, tag=None):
+            return sb.tile(shape, dtype, name=name, tag=tag or name, align_bytes=64)
 
         def load_list(name, src):
             lst = sb.tile(list(src.shape), U16, name=name)
@@ -46,9 +46,9 @@ def tile_list_crossed_board_skip_bestoftwo_kernel(
                 rows = rows.rearrange("p n t -> p (n t)")
             queue.dma_start(dst.bitcast(I32), rows.bitcast(I32))
 
-        def load_scales(dst, src):
+        def load_scales(dst, src, quads=range(QUADS)):
             rows = src[0].bitcast(I32)
-            for q in range(QUADS):
+            for q in quads:
                 nc.sync.dma_start(dst[32 * q : 32 * q + 4, :].bitcast(I32), rows[4 * q : 4 * q + 4, :])
 
         xt_w = tile("xt_w", [P, T], U32)
@@ -57,129 +57,163 @@ def tile_list_crossed_board_skip_bestoftwo_kernel(
         xo_s = tile("xo_s", [P, Z], U8)
         w_raw = tile("w_raw", [P, R], U32)
         w2_raw = tile("w2_raw", [P, R], U32)
-        ws1_raw = tile("ws1_raw", [P, 2 * R], U8)
-        s2 = tile("s2", [P, 3 * N], U8)
+        ws1_raw = tile("ws1_raw", [P, 2 * R + 2 * J], U8)
         boards = [tile("board%d" % t, [P, C], F32) for t in range(PACK)]
 
-        for plane in (xt_s, xo_s, ws1_raw, s2):
-            nc.vector.memset(plane[:].bitcast(I32), 0)
-        for board in boards:
-            nc.vector.memset(board[:], 0.0)
+        staged = tile("staged", [P, 2 * R + 2 * J], U8)
+        for window in (xt_s, xo_s):
+            nc.vector.memset(window[0:96, :].bitcast(I32), 0)
+        nc.vector.memset(ws1_raw[:].bitcast(I32), 0)
+        for t, board in enumerate(boards):
+            (nc.vector, nc.gpsimd)[t // 2].memset(board[:], 0.0)
+
+        def load_window(dst, src):
+            rows = src[0].bitcast(I32)
+            nc.sync.dma_start(dst[96:P, :].bitcast(I32), rows.unsqueeze(1).to_broadcast([16, 2, rows.shape[1]]))
 
         l1 = load_list("l1", offs)
+        load_window(xt_s, xt_scales)
         l2 = load_list("l2", offs2)
-        load_words(nc.scalar, xt_w[:], xt_words)
-        load_words(nc.scalar, xo_w[:], xo_words)
-        load_words(nc.scalar, w_raw[:], w_words)
-        load_words(nc.scalar, w2_raw[:], w2_words)
-        load_scales(xt_s, xt_scales)
-        load_scales(xo_s, xo_scales)
-        load_scales(ws1_raw[:, 0:R], w_scales)
-        load_scales(ws1_raw[:, R : 2 * R], w2_scales)
+        load_window(xo_s, xo_scales)
+        for u, src in enumerate((w_scales, w2_scales)):
+            nc.sync.dma_start(staged[96:P:2, u * R : (u + 1) * R].bitcast(I32), src[0].bitcast(I32))
+        load_words(nc.sync, w_raw[:], w_words)
+        load_words(nc.sync, xt_w[:], xt_words)
         l3 = load_list("l3", offs3)
         l4 = load_list("l4", offs4)
-        wb_w = tile("wb_w", [P, N], U32)
-        ws_w = tile("ws_w", [P, N], U32)
-        sx_w = tile("sx_w", [P, J], U16)
-        wb_s, ws_s, sx_s = s2[:, 0:N], s2[:, N : 2 * N], s2[:, 2 * N : 3 * N]
-        load_words(nc.sync, sx_w[:], sx_words)
-        load_words(nc.sync, ws_w[:], ws_words)
-        load_scales(sx_s, sx_scales)
-        load_scales(ws_s, ws_scales)
-        load_words(nc.sync, wb_w[:], wb_words)
-        load_scales(wb_s, wb_scales)
+        load_words(nc.sync, xo_w[:], xo_words)
+        load_words(nc.sync, w2_raw[:], w2_words)
         l5 = load_list("l5", offs5)
         l6 = load_list("l6", offs6)
-
         xt_gs = tile("xt_gs", [P, J], U8)
-        xt_gw = tile("xt_gw", [P, J], U32)
         xo_gs = tile("xo_gs", [P, J], U8)
+        xt_ms, xo_ms = ws1_raw[:, 2 * R : 2 * R + J], ws1_raw[:, 2 * R + J : 2 * R + 2 * J]
+        nc.vector.tensor_copy(xt_gs[:], xt_s[:].indirect(l1[:]))
+        nc.vector.tensor_copy(xo_gs[:], xo_s[:].indirect(l2[:]))
+        nc.vector.tensor_copy(staged[:, 2 * R : 2 * R + J].bitcast(I32), xt_gs[:].bitcast(I32))
+        nc.vector.tensor_copy(staged[:, 2 * R + J : 2 * R + 2 * J].bitcast(I32), xo_gs[:].bitcast(I32))
+        for q in range(QUADS):
+            nc.sync.dma_start(ws1_raw[32 * q : 32 * q + 4, :].bitcast(I32), staged[96 + 8 * q : 104 + 8 * q : 2, :].bitcast(I32))
+
+        xt_gw = tile("xt_gw", [P, J], U32)
         xo_gw = tile("xo_gw", [P, J], U16)
         w_w = tile("w_w", [P, R], U32)
         w2_w = tile("w2_w", [P, R], U32)
-        w_s = tile("w_s", [P, R], U8)
-        w2_s = tile("w2_s", [P, R], U8)
+        s1 = [tile("s1_%d" % t, [P, 2, P], U8) for t in range(PACK)]
+        order = range(PACK)
 
-        def deal(copy, dst, src):
-            copy(dst.rearrange("p (t m) -> p t m", t=PACK), src.rearrange("p (m t) -> p t m", t=PACK))
-
+        nc.scalar.copy(w_w[:].rearrange("p (t m) -> p t m", t=PACK), w_raw[:].rearrange("p (m t) -> p t m", t=PACK))
         nc.vector.tensor_copy(xt_gw[:], xt_w[:].indirect(l1[:]))
         nc.vector.tensor_copy(xo_gw[:], xo_w[:].indirect(l2[:]))
-        nc.vector.tensor_copy(xt_gs[:], xt_s[:].indirect(l1[:]))
-        deal(nc.scalar.copy, w_w[:], w_raw[:])
-        deal(nc.vector.tensor_copy, w2_w[:], w2_raw[:])
-        nc.vector.tensor_copy(xo_gs[:], xo_s[:].indirect(l2[:]))
-        deal(nc.vector.tensor_copy, w_s[:], ws1_raw[:, 0:R])
-        deal(nc.vector.tensor_copy, w2_s[:], ws1_raw[:, R : 2 * R])
+        nc.scalar.copy(w2_w[:].rearrange("p (t m) -> p t m", t=PACK), w2_raw[:].rearrange("p (m t) -> p t m", t=PACK))
+        for t in order:
+            for u in range(2):
+                nc.vector.tensor_copy(s1[t][:, u, :], ws1_raw[:, u * R + t : (u + 1) * R : PACK])
 
-        xt_op = (xt_gw[:].bitcast(E4M3), xt_gs[:])
-        xo_op = (xo_gw[:].bitcast(E2M1), xo_gs[:])
+        late = tile("late", [P, 8 * N + 2 * J + 3 * N], U8, tag="w2_raw")
+        ws_w, wb_w = late[:, 0 : 4 * N].bitcast(U32), late[:, 4 * N : 8 * N].bitcast(U32)
+        sx_w, s2 = late[:, 8 * N : 8 * N + 2 * J], late[:, 8 * N + 2 * J : 8 * N + 2 * J + 3 * N]
+        wb_s, ws_s, sx_s = s2[:, 0:N], s2[:, N : 2 * N], s2[:, 2 * N : 3 * N]
+        nc.vector.memset(s2.bitcast(I32), 0)
+        load_words(nc.sync, ws_w, ws_words)
+        load_words(nc.sync, wb_w, wb_words)
+        load_words(nc.sync, sx_w, sx_words)
+        load_scales(sx_s, sx_scales)
+        load_scales(ws_s, ws_scales)
+        load_scales(wb_s, wb_scales)
 
-        def mm(dst, words, scales, col0, moving, start, stop):
-            cols = slice(col0, col0 + P)
+        xt_op = (xt_gw[:].bitcast(E4M3), xt_ms)
+        xo_op = (xo_gw[:].bitcast(E2M1), xo_ms)
+
+        def mm(dst, words, scales, moving, start, stop):
             nc.tensor.matmul_mx(
-                out=dst, lhsT=words[:, cols].bitcast(E5M2), lhsT_scale=scales[:, cols],
+                out=dst, lhsT=words.bitcast(E5M2), lhsT_scale=scales,
                 rhs=moving[0], rhs_scale=moving[1], start=start, stop=stop,
             )
 
-        order = (0, 2, 1, 3)
-        a_ps = [ps.tile([P, J], F32, name="a_ps%d" % t) for t in range(PACK)]
+        def cols(i):
+            return slice(i * P, (i + 1) * P)
+
+        a_ps = [ps.tile([P, J], F32, name="a_ps%d" % t, tag="a_ps%d" % t) for t in range(PACK)]
         b_ps = [ps.tile([P, 2, J], F32, name="b_ps%d" % h) for h in range(2)]
-        p_ps = [ps.tile([P, J], F32, name="p_ps%d" % h) for h in range(2)]
         for t in order:
-            mm(a_ps[t][:], w_w, w_s, t * P, xt_op, True, False)
-        for t in order:
-            mm(a_ps[t][:], w2_w, w2_s, t * P, xo_op, False, True)
+            mm(a_ps[t][:], w_w[:, cols(t)], s1[t][:, 0, :], xt_op, True, False)
+            mm(a_ps[t][:], w2_w[:, cols(t)], s1[t][:, 1, :], xo_op, False, True)
         for t in range(PACK):
-            mm(b_ps[t // 2][:, t % 2, :], w2_w, w2_s, t * P, xt_op, True, False)
-            mm(b_ps[t // 2][:, t % 2, :], w_w, w_s, t * P, xo_op, False, True)
-        sx_op = (sx_w[:].bitcast(E2M1), sx_s)
-        for h in range(2):
-            mm(p_ps[h][:], ws_w, ws_s, h * P, sx_op, True, False)
+            mm(b_ps[t // 2][:, t % 2, :], w2_w[:, cols(t)], s1[t][:, 1, :], xt_op, True, False)
+            mm(b_ps[t // 2][:, t % 2, :], w_w[:, cols(t)], s1[t][:, 0, :], xo_op, False, True)
 
         a_sb = [tile("a_sb%d" % t, [P, J], F32) for t in range(PACK)]
         got = [tile("got%d" % h, [P, 2, J], F32) for h in range(2)]
         hid = tile("hid", [P, J, PACK], BF16)
 
-        def larger(h):
+        def larger(h, js):
             nc.vector.tensor_tensor(
-                hid[:, :, 2 * h : 2 * h + 2],
-                got[h][:].rearrange("p t j -> p j t"),
-                b_ps[h][:].rearrange("p t j -> p j t"),
+                hid[:, js, 2 * h : 2 * h + 2],
+                got[h][:, :, js].rearrange("p t j -> p j t"),
+                b_ps[h][:, :, js].rearrange("p t j -> p j t"),
                 MAX,
             )
 
-        for t in (0, 2, 1):
-            nc.scalar.activation(a_sb[t][:], a_ps[t][:], COPY)
-        nc.vector.tensor_copy(boards[0][:].indirect(l3[:]), a_sb[0][:])
-        nc.scalar.activation(boards[2][:].indirect(l3[:]), a_sb[2][:], COPY)
-        nc.vector.tensor_copy(boards[1][:].indirect(l3[:]), a_sb[1][:])
-        nc.scalar.activation(a_sb[3][:], a_ps[3][:], COPY)
-        nc.scalar.activation(boards[3][:].indirect(l3[:]), a_sb[3][:], COPY)
-        for t in (0, 1):
-            nc.vector.tensor_copy(got[0][:, t, :], boards[t][:].indirect(l4[:]))
-        for t in (2, 3):
-            nc.scalar.activation(got[1][:, t - 2, :], boards[t][:].indirect(l4[:]), COPY)
-        larger(0)
-        larger(1)
+        def put(t):
+            if t % 2 == 0:
+                nc.vector.tensor_copy(boards[t][:].indirect(l3[:]), a_sb[t][:])
+            else:
+                nc.scalar.activation(boards[t][:].indirect(l3[:]), a_sb[t][:], COPY)
 
-        hid_w = tile("hid_w", [P, J], U32)
-        hid_s = tile("hid_s", [P, J], U8)
-        nc.vector.quantize_mx(out=hid_w[:].bitcast(E4M3), scales=hid_s[:], in_=hid[:].rearrange("p j t -> p (j t)"))
-        hid_op = (hid_w[:].bitcast(E4M3), hid_s[:])
-        for h in range(2):
-            mm(p_ps[h][:], wb_w, wb_s, h * P, hid_op, False, True)
+        def fetch(t, u0, u1):
+            dst = got[t // 2][:, t % 2, u0 * P : u1 * P]
+            src = boards[t][:].indirect(l4[:, u0 * 8 : u1 * 8])
+            if t % 2 == 0:
+                nc.vector.tensor_copy(dst, src)
+            else:
+                nc.scalar.activation(dst, src, COPY)
+
+        for t in (0, 1):
+            nc.scalar.activation(a_sb[t][:], a_ps[t][:], COPY)
+        put(0)
+        put(1)
+        nc.vector.tensor_copy(a_sb[2][:], a_ps[2][:])
+        nc.scalar.activation(a_sb[3][:], a_ps[3][:], COPY)
+        fetch(0, 0, 2)
+        fetch(1, 0, 2)
+        put(2)
+        put(3)
+        larger(0, slice(0, J))
+        for u in range(2):
+            fetch(2, u, u + 1)
+            fetch(3, u, u + 1)
+        for u in range(2):
+            larger(1, cols(u))
+
+        tags = {(0, 0): "p00", (1, 0): "p10", (0, 1): "a_ps0", (1, 1): "a_ps1"}
+        p_ps = {(h, u): ps.tile([P, P], F32, name="p_ps%d%d" % (h, u), tag=tags[h, u]) for u in range(2) for h in range(2)}
+        for u in range(2):
+            sx_op = (sx_w[:, 2 * u * P : 2 * (u + 1) * P].bitcast(E2M1), sx_s[:, cols(u)])
+            for h in range(2):
+                mm(p_ps[h, u][:], ws_w[:, cols(h)], ws_s[:, cols(h)], sx_op, True, False)
+        hid_w = [tile("hid_w%d" % u, [P, P], U32) for u in range(2)]
+        hid_s = [tile("hid_s%d" % u, [P, P], U8) for u in range(2)]
+        for u in range(2):
+            nc.vector.quantize_mx(
+                out=hid_w[u][:].bitcast(E4M3), scales=hid_s[u][:], in_=hid[:, cols(u), :].rearrange("p j t -> p (j t)")
+            )
+        for u in range(2):
+            for h in range(2):
+                mm(p_ps[h, u][:], wb_w[:, cols(h)], wb_s[:, cols(h)], (hid_w[u][:].bitcast(E4M3), hid_s[u][:]), False, True)
 
         p_sb = [tile("p_sb%d" % h, [P, J], F32) for h in range(2)]
         first = [tile("first%d" % h, [P, E], F32) for h in range(2)]
         second = [tile("second%d" % h, [P, E], F32) for h in range(2)]
         best = [tile("best%d" % h, [P, E], F32) for h in range(2)]
-        nc.scalar.activation(p_sb[0][:], p_ps[0][:], COPY)
-        nc.vector.tensor_copy(p_sb[1][:], p_ps[1][:])
-        nc.scalar.activation(first[0][:], p_sb[0][:].indirect(l5[:]), COPY)
-        nc.scalar.activation(second[0][:], p_sb[0][:].indirect(l6[:]), COPY)
-        nc.vector.tensor_copy(first[1][:], p_sb[1][:].indirect(l5[:]))
-        nc.vector.tensor_copy(second[1][:], p_sb[1][:].indirect(l6[:]))
-        for h, queue in ((0, nc.scalar), (1, nc.sync)):
+        for h in range(2):
+            nc.scalar.activation(p_sb[h][:, cols(0)], p_ps[h, 0][:], COPY)
+        nc.vector.tensor_copy(p_sb[0][:, cols(1)], p_ps[0, 1][:])
+        nc.scalar.activation(p_sb[1][:, cols(1)], p_ps[1, 1][:], COPY)
+        nc.vector.tensor_copy(first[0][:], p_sb[0][:].indirect(l5[:]))
+        nc.vector.tensor_copy(second[0][:], p_sb[0][:].indirect(l6[:]))
+        nc.scalar.activation(first[1][:], p_sb[1][:].indirect(l5[:]), COPY)
+        nc.scalar.activation(second[1][:], p_sb[1][:].indirect(l6[:]), COPY)
+        for h, queue in ((0, nc.sync), (1, nc.scalar)):
             nc.vector.tensor_tensor(best[h][:], first[h][:], second[h][:], MAX)
             queue.dma_start(out[h * P : (h + 1) * P, :], best[h][:])

@@ -78,10 +78,10 @@ def tile_list_crossed_board_skip_bestoftwo_kernel(
         for u, src in enumerate((w_scales, w2_scales)):
             nc.sync.dma_start(staged[96:P:2, u * R : (u + 1) * R].bitcast(I32), src[0].bitcast(I32))
         load_words(nc.sync, w_raw[:], w_words)
-        load_words(nc.sync, xt_w[:], xt_words)
+        load_words(nc.sync, xo_w[:], xo_words)
         l3 = load_list("l3", offs3)
         l4 = load_list("l4", offs4)
-        load_words(nc.sync, xo_w[:], xo_words)
+        load_words(nc.sync, xt_w[:], xt_words)
         load_words(nc.sync, w2_raw[:], w2_words)
         l5 = load_list("l5", offs5)
         l6 = load_list("l6", offs6)
@@ -102,10 +102,10 @@ def tile_list_crossed_board_skip_bestoftwo_kernel(
         s1 = [tile("s1_%d" % t, [P, 2, P], U8) for t in range(PACK)]
         order = range(PACK)
 
-        nc.scalar.copy(w_w[:].rearrange("p (t m) -> p t m", t=PACK), w_raw[:].rearrange("p (m t) -> p t m", t=PACK))
-        nc.vector.tensor_copy(xt_gw[:], xt_w[:].indirect(l1[:]))
+        nc.scalar.copy(w_w[:].rearrange("p (t c i) -> p c t i", t=PACK, i=4), w_raw[:].rearrange("p (c i t) -> p c t i", t=PACK, i=4))
         nc.vector.tensor_copy(xo_gw[:], xo_w[:].indirect(l2[:]))
-        nc.scalar.copy(w2_w[:].rearrange("p (t m) -> p t m", t=PACK), w2_raw[:].rearrange("p (m t) -> p t m", t=PACK))
+        nc.vector.tensor_copy(xt_gw[:], xt_w[:].indirect(l1[:]))
+        nc.vector.tensor_copy(w2_w[:].rearrange("p (t c i) -> p c t i", t=PACK, i=4), w2_raw[:].rearrange("p (c i t) -> p c t i", t=PACK, i=4))
         for t in order:
             for u in range(2):
                 nc.vector.tensor_copy(s1[t][:, u, :], ws1_raw[:, u * R + t : (u + 1) * R : PACK])

from contextlib import ExitStack

import concourse.mybir as mybir

K, T, Z, J, R, C, N, L, E = 512, 1024, 1024, 256, 512, 512, 256, 512, 128
FLOPS = 2 * J * (4 * K * R + R * N + L * N)

F32 = mybir.dt.float32
BF16 = mybir.dt.bfloat16
I32 = mybir.dt.int32
U32 = mybir.dt.uint32
U16 = mybir.dt.uint16
U8 = mybir.dt.uint8
E4M3 = mybir.dt.float8_e4m3fn_x4
E5M2 = mybir.dt.float8_e5m2_x4
E2M1 = mybir.dt.float4_e2m1fn_x4
COPY = mybir.ActivationFunctionType.Copy
MAX = mybir.AluOpType.max

P = 128
PACK = 4
QUADS = 4


def tile_list_crossed_board_skip_bestoftwo_kernel(
    tc, xt_words, xt_scales, xo_words, xo_scales, w_words, w_scales, w2_words, w2_scales,
    wb_words, wb_scales, sx_words, sx_scales, ws_words, ws_scales,
    offs, offs2, offs3, offs4, offs5, offs6, out,
):
    nc = tc.nc
    with ExitStack() as ctx:
        sb = ctx.enter_context(tc.tile_pool(name="sb", bufs=1))
        ps = ctx.enter_context(tc.psum_pool(name="ps", bufs=1))

        def tile(name, shape, dtype, tag=None):
            return sb.tile(shape, dtype, name=name, tag=tag or name, align_bytes=64)

        def load_list(name, src):
            lst = sb.tile(list(src.shape), U16, name=name)
            nc.sync.dma_start(lst[:], src)
            return lst

        def load_words(queue, dst, src):
            rows = src[0]
            if len(rows.shape) == 3:
                rows = rows.rearrange("p n t -> p (n t)")
            queue.dma_start(dst.bitcast(I32), rows.bitcast(I32))

        def load_scales(dst, src, quads=range(QUADS)):
            rows = src[0].bitcast(I32)
            for q in quads:
                nc.sync.dma_start(dst[32 * q : 32 * q + 4, :].bitcast(I32), rows[4 * q : 4 * q + 4, :])

        xt_w = tile("xt_w", [P, T], U32)
        xt_s = tile("xt_s", [P, T], U8)
        xo_w = tile("xo_w", [P, Z], U16)
        xo_s = tile("xo_s", [P, Z], U8)
        w_raw = tile("w_raw", [P, R], U32)
        w2_raw = tile("w2_raw", [P, R], U32)
        ws1_raw = tile("ws1_raw", [P, 2 * R + 2 * J], U8)
        boards = [tile("board%d" % t, [P, C], F32) for t in range(PACK)]

        staged = tile("staged", [P, 2 * R + 2 * J], U8)
        for window in (xt_s, xo_s):
            nc.vector.memset(window[0:96, :].bitcast(I32), 0)
        nc.vector.memset(ws1_raw[:].bitcast(I32), 0)
        for t, board in enumerate(boards):
            (nc.vector, nc.gpsimd)[t // 2].memset(board[:], 0.0)

        def load_window(dst, src):
            rows = src[0].bitcast(I32)
            nc.sync.dma_start(dst[96:P, :].bitcast(I32), rows.unsqueeze(1).to_broadcast([16, 2, rows.shape[1]]))

        l1 = load_list("l1", offs)
        load_window(xt_s, xt_scales)
        l2 = load_list("l2", offs2)
        load_window(xo_s, xo_scales)
        for u, src in enumerate((w_scales, w2_scales)):
            nc.sync.dma_start(staged[96:P:2, u * R : (u + 1) * R].bitcast(I32), src[0].bitcast(I32))
        load_words(nc.sync, w_raw[:], w_words)
        load_words(nc.sync, xo_w[:], xo_words)
        l3 = load_list("l3", offs3)
        l4 = load_list("l4", offs4)
        load_words(nc.sync, xt_w[:], xt_words)
        load_words(nc.sync, w2_raw[:], w2_words)
        l5 = load_list("l5", offs5)
        l6 = load_list("l6", offs6)
        xt_gs = tile("xt_gs", [P, J], U8)
        xo_gs = tile("xo_gs", [P, J], U8)
        xt_ms, xo_ms = ws1_raw[:, 2 * R : 2 * R + J], ws1_raw[:, 2 * R + J : 2 * R + 2 * J]
        nc.vector.tensor_copy(xt_gs[:], xt_s[:].indirect(l1[:]))
        nc.vector.tensor_copy(xo_gs[:], xo_s[:].indirect(l2[:]))
        nc.vector.tensor_copy(staged[:, 2 * R : 2 * R + J].bitcast(I32), xt_gs[:].bitcast(I32))
        nc.vector.tensor_copy(staged[:, 2 * R + J : 2 * R + 2 * J].bitcast(I32), xo_gs[:].bitcast(I32))
        for q in range(QUADS):
            nc.sync.dma_start(ws1_raw[32 * q : 32 * q + 4, :].bitcast(I32), staged[96 + 8 * q : 104 + 8 * q : 2, :].bitcast(I32))

        xt_gw = tile("xt_gw", [P, J], U32)
        xo_gw = tile("xo_gw", [P, J], U16)
        w_w = tile("w_w", [P, R], U32)
        w2_w = tile("w2_w", [P, R], U32)
        s1 = [tile("s1_%d" % t, [P, 2, P], U8) for t in range(PACK)]
        order = range(PACK)

        nc.scalar.copy(w_w[:].rearrange("p (t c i) -> p c t i", t=PACK, i=4), w_raw[:].rearrange("p (c i t) -> p c t i", t=PACK, i=4))
        nc.vector.tensor_copy(xo_gw[:], xo_w[:].indirect(l2[:]))
        nc.vector.tensor_copy(xt_gw[:], xt_w[:].indirect(l1[:]))
        nc.vector.tensor_copy(w2_w[:].rearrange("p (t c i) -> p c t i", t=PACK, i=4), w2_raw[:].rearrange("p (c i t) -> p c t i", t=PACK, i=4))
        for t in order:
            for u in range(2):
                nc.vector.tensor_copy(s1[t][:, u, :], ws1_raw[:, u * R + t : (u + 1) * R : PACK])

        late = tile("late", [P, 8 * N + 2 * J + 3 * N], U8, tag="w2_raw")
        ws_w, wb_w = late[:, 0 : 4 * N].bitcast(U32), late[:, 4 * N : 8 * N].bitcast(U32)
        sx_w, s2 = late[:, 8 * N : 8 * N + 2 * J], late[:, 8 * N + 2 * J : 8 * N + 2 * J + 3 * N]
        wb_s, ws_s, sx_s = s2[:, 0:N], s2[:, N : 2 * N], s2[:, 2 * N : 3 * N]
        nc.vector.memset(s2.bitcast(I32), 0)
        load_words(nc.sync, ws_w, ws_words)
        load_words(nc.sync, wb_w, wb_words)
        load_words(nc.sync, sx_w, sx_words)
        load_scales(sx_s, sx_scales)
        load_scales(ws_s, ws_scales)
        load_scales(wb_s, wb_scales)

        xt_op = (xt_gw[:].bitcast(E4M3), xt_ms)
        xo_op = (xo_gw[:].bitcast(E2M1), xo_ms)

        def mm(dst, words, scales, moving, start, stop):
            nc.tensor.matmul_mx(
                out=dst, lhsT=words.bitcast(E5M2), lhsT_scale=scales,
                rhs=moving[0], rhs_scale=moving[1], start=start, stop=stop,
            )

        def cols(i):
            return slice(i * P, (i + 1) * P)

        a_ps = [ps.tile([P, J], F32, name="a_ps%d" % t, tag="a_ps%d" % t) for t in range(PACK)]
        b_ps = [ps.tile([P, 2, J], F32, name="b_ps%d" % h) for h in range(2)]
        for t in order:
            mm(a_ps[t][:], w_w[:, cols(t)], s1[t][:, 0, :], xt_op, True, False)
            mm(a_ps[t][:], w2_w[:, cols(t)], s1[t][:, 1, :], xo_op, False, True)
        for t in range(PACK):
            mm(b_ps[t // 2][:, t % 2, :], w2_w[:, cols(t)], s1[t][:, 1, :], xt_op, True, False)
            mm(b_ps[t // 2][:, t % 2, :], w_w[:, cols(t)], s1[t][:, 0, :], xo_op, False, True)

        a_sb = [tile("a_sb%d" % t, [P, J], F32) for t in range(PACK)]
        got = [tile("got%d" % h, [P, 2, J], F32) for h in range(2)]
        hid = tile("hid", [P, J, PACK], BF16)

        def larger(h, js):
            nc.vector.tensor_tensor(
                hid[:, js, 2 * h : 2 * h + 2],
                got[h][:, :, js].rearrange("p t j -> p j t"),
                b_ps[h][:, :, js].rearrange("p t j -> p j t"),
                MAX,
            )

        def put(t):
            if t % 2 == 0:
                nc.vector.tensor_copy(boards[t][:].indirect(l3[:]), a_sb[t][:])
            else:
                nc.scalar.activation(boards[t][:].indirect(l3[:]), a_sb[t][:], COPY)

        def fetch(t, u0, u1):
            dst = got[t // 2][:, t % 2, u0 * P : u1 * P]
            src = boards[t][:].indirect(l4[:, u0 * 8 : u1 * 8])
            if t % 2 == 0:
                nc.vector.tensor_copy(dst, src)
            else:
                nc.scalar.activation(dst, src, COPY)

        for t in (0, 1):
            nc.scalar.activation(a_sb[t][:], a_ps[t][:], COPY)
        put(0)
        put(1)
        nc.vector.tensor_copy(a_sb[2][:], a_ps[2][:])
        nc.scalar.activation(a_sb[3][:], a_ps[3][:], COPY)
        fetch(0, 0, 2)
        fetch(1, 0, 2)
        put(2)
        put(3)
        larger(0, slice(0, J))
        for u in range(2):
            fetch(2, u, u + 1)
            fetch(3, u, u + 1)
        for u in range(2):
            larger(1, cols(u))

        tags = {(0, 0): "p00", (1, 0): "p10", (0, 1): "a_ps0", (1, 1): "a_ps1"}
        p_ps = {(h, u): ps.tile([P, P], F32, name="p_ps%d%d" % (h, u), tag=tags[h, u]) for u in range(2) for h in range(2)}
        for u in range(2):
            sx_op = (sx_w[:, 2 * u * P : 2 * (u + 1) * P].bitcast(E2M1), sx_s[:, cols(u)])
            for h in range(2):
                mm(p_ps[h, u][:], ws_w[:, cols(h)], ws_s[:, cols(h)], sx_op, True, False)
        hid_w = [tile("hid_w%d" % u, [P, P], U32) for u in range(2)]
        hid_s = [tile("hid_s%d" % u, [P, P], U8) for u in range(2)]
        for u in range(2):
            nc.vector.quantize_mx(
                out=hid_w[u][:].bitcast(E4M3), scales=hid_s[u][:], in_=hid[:, cols(u), :].rearrange("p j t -> p (j t)")
            )
        for u in range(2):
            for h in range(2):
                mm(p_ps[h, u][:], wb_w[:, cols(h)], wb_s[:, cols(h)], (hid_w[u][:].bitcast(E4M3), hid_s[u][:]), False, True)

        p_sb = [tile("p_sb%d" % h, [P, J], F32) for h in range(2)]
        first = [tile("first%d" % h, [P, E], F32) for h in range(2)]
        second = [tile("second%d" % h, [P, E], F32) for h in range(2)]
        best = [tile("best%d" % h, [P, E], F32) for h in range(2)]
        for h in range(2):
            nc.scalar.activation(p_sb[h][:, cols(0)], p_ps[h, 0][:], COPY)
        nc.vector.tensor_copy(p_sb[0][:, cols(1)], p_ps[0, 1][:])
        nc.scalar.activation(p_sb[1][:, cols(1)], p_ps[1, 1][:], COPY)
        nc.vector.tensor_copy(first[0][:], p_sb[0][:].indirect(l5[:]))
        nc.vector.tensor_copy(second[0][:], p_sb[0][:].indirect(l6[:]))
        nc.scalar.activation(first[1][:], p_sb[1][:].indirect(l5[:]), COPY)
        nc.scalar.activation(second[1][:], p_sb[1][:].indirect(l6[:]), COPY)
        for h, queue in ((0, nc.sync), (1, nc.scalar)):
            nc.vector.tensor_tensor(best[h][:], first[h][:], second[h][:], MAX)
            queue.dma_start(out[h * P : (h + 1) * P, :], best[h][:])
